import numpy as np
import ml_dtypes


def mxq(x, axis, fmt="e4m3"):
    dtype, down = {"e4m3": (ml_dtypes.float8_e4m3fn, 7), "e5m2": (ml_dtypes.float8_e5m2, 14)}[fmt]
    v = np.moveaxis(np.asarray(x, np.float32).astype(ml_dtypes.bfloat16).astype(np.float64), axis, -1)
    blocks = v.reshape(v.shape[:-1] + (-1, 32))
    amax = np.abs(blocks).max(-1, keepdims=True)
    byte = np.maximum(np.where(amax > 0, np.frexp(amax)[1] - 1 + 127, 0) - down, 1)
    scale = np.exp2(byte - 127.0)
    codes = (blocks / scale).astype(np.float32).astype(dtype).astype(np.float64)
    return np.moveaxis((codes * scale).reshape(v.shape), -1, axis)


WIDE = False


def mx_kscale(k):
    if not WIDE:
        return np.ones(k)
    levels = np.array([30, -30])
    if k % 512:
        return np.exp2(np.random.permutation(np.resize(levels, k // 32))).repeat(32)
    a = np.empty((k // 512, 16))
    for p in range(k // 512):
        a[p, :8] = np.random.permutation(np.resize(levels, 8))
        for g in range(8):
            far = levels[np.abs(levels - a[p, g]) >= 10]
            a[p, g + 8] = far[np.random.randint(len(far))]
    return np.exp2(a.ravel()).repeat(32)


def f64(x):
    return np.asarray(x).astype(np.float64)


def striped(idx):
    return np.tile(np.asarray(idx).reshape(-1, 16).T, (8, 1)).astype(np.uint16)


def unstriped(offs):
    return offs[:16].T.reshape(-1).astype(np.int64)


E2M1 = np.array([0.0, 0.5, 1.0, 1.5, 2.0, 3.0, 4.0, 6.0, -0.0, -0.5, -1.0, -1.5, -2.0, -3.0, -4.0, -6.0])


def pack_weight(w, fmt):
    k, n = w.shape
    w = f64(np.asarray(w, np.float32).astype(ml_dtypes.bfloat16)).reshape(k // 32, 32, n)
    amax = np.abs(w).max(1)
    if fmt in ("e4m3", "e5m2"):
        byte = np.frexp(amax)[1] - 1 + 127 - (7 if fmt == "e4m3" else 14)
    else:
        mant, ex = np.frexp(amax / 6.0)
        byte = np.where(mant > 0.5, ex, ex - 1) + 127
    byte = np.clip(np.where(amax > 0, byte, 1), 1, 254)
    scaled = (w * np.exp2(127.0 - byte)[:, None, :]).reshape(k, n).astype(np.float32)
    by_word = np.ascontiguousarray(scaled.reshape(k // 512, 128, 4, n).transpose(0, 1, 3, 2))
    if fmt in ("e4m3", "e5m2"):
        words = by_word.astype(ml_dtypes.float8_e4m3fn if fmt == "e4m3" else ml_dtypes.float8_e5m2).view(np.uint8)
    else:
        c = by_word.astype(ml_dtypes.float4_e2m1fn).view(np.uint8) & 0xF
        words = (c[..., 0::2] | (c[..., 1::2] << 4)).reshape(k // 512, 128, 2 * n)
    return np.ascontiguousarray(words), np.ascontiguousarray(byte.astype(np.uint8).reshape(k // 512, 16, n))


def unpack_weight(words, scales, fmt):
    g, _, n = scales.shape
    words = np.ascontiguousarray(words).reshape(g, 128, n, -1)
    if fmt in ("e4m3", "e5m2"):
        vals = words.view(ml_dtypes.float8_e4m3fn if fmt == "e4m3" else ml_dtypes.float8_e5m2).astype(np.float64)
    else:
        nib = np.empty((g, 128, n, 4), np.uint8)
        nib[..., 0::2] = words & 0xF
        nib[..., 1::2] = words >> 4
        vals = E2M1[nib]
    vals = vals * np.repeat(np.exp2(scales.astype(np.float64) - 127.0), 8, axis=1)[..., None]
    return vals.transpose(0, 1, 3, 2).reshape(g * 512, n)


def sigmoid(v):
    return 1.0 / (1.0 + np.exp(-v))


K, T, Z, J, R, C, O, N, E = 512, 1024, 1024, 256, 512, 512, 256, 256, 1024


def setup_inputs():
    n = np.random.standard_normal
    idx = np.random.permutation(T)[:J]
    idx2 = np.random.permutation(Z)[:J]
    idx3 = np.random.permutation(C)[:J]
    idx4 = np.random.permutation(C)[:J]
    idx5 = np.random.permutation(C)[:O]
    idx6 = np.random.permutation(C)[:O]
    idx7 = np.random.permutation(E)[:O]
    fk = mx_kscale(K)
    fr = mx_kscale(R)
    xtp = pack_weight(n((K, T)) / fk[:, None], "e2m1")
    xop = pack_weight(n((K, Z)) / fk[:, None], "e4m3")
    wp = pack_weight(n((K, R)) * 1 / np.sqrt(K) * fk[:, None] * fr, "e4m3")
    w2p = pack_weight(n((K, R)) * 1 / np.sqrt(K) * fk[:, None] * fr, "e5m2")
    wbp = pack_weight(n((R, N)) * 1 / np.sqrt(R) / fr[:, None], "e2m1")
    return {
        "xt_words": xtp[0],
        "xt_scales": xtp[1],
        "xo_words": xop[0],
        "xo_scales": xop[1],
        "w_words": wp[0],
        "w_scales": wp[1],
        "w2_words": w2p[0],
        "w2_scales": w2p[1],
        "wb_words": wbp[0],
        "wb_scales": wbp[1],
        "tz": (n((N, E))).astype(np.float32),
        "so": (np.random.uniform(0.6, 1.6, (N, 1))).astype(np.float32),
        "bo": (np.random.uniform(-1.0, 1.0, (N, 1))).astype(np.float32),
        "offs": striped(idx),
        "offs2": striped(idx2),
        "offs3": striped(idx3),
        "offs4": striped(idx4),
        "offs5": striped(idx5),
        "offs6": striped(idx6),
        "offs7": striped(idx7),
    }


def reference(xt_words, xt_scales, xo_words, xo_scales, w_words, w_scales, w2_words, w2_scales, wb_words, wb_scales, tz, so, bo, offs, offs2, offs3, offs4, offs5, offs6, offs7):
    idx = unstriped(offs)
    idx2 = unstriped(offs2)
    idx3 = unstriped(offs3)
    idx4 = unstriped(offs4)
    idx5 = unstriped(offs5)
    idx6 = unstriped(offs6)
    idx7 = unstriped(offs7)
    xtu = unpack_weight(xt_words, xt_scales, "e2m1")
    xou = unpack_weight(xo_words, xo_scales, "e4m3")
    wu = unpack_weight(w_words, w_scales, "e4m3")
    w2u = unpack_weight(w2_words, w2_scales, "e5m2")
    wbu = unpack_weight(wb_words, wb_scales, "e2m1")
    xtidxg = xtu[:, idx]
    xoidx2g = xou[:, idx2]
    a = wu.T @ xtidxg + w2u.T @ xoidx2g
    b = w2u.T @ xtidxg + wu.T @ xoidx2g
    pw = np.zeros((R, C))
    pw[:, idx3] = a
    pv = np.zeros((R, C))
    pv[:, idx4] = b
    hid = np.abs(pw[:, idx5] - pv[:, idx6])
    hidq = mxq(hid, 0, "e5m2")
    p = wbu.T @ hidq
    y = p * sigmoid(f64(tz)[:, idx7] * f64(so) + f64(bo))
    return y

@@ -1,0 +1,227 @@
+from contextlib import ExitStack
+
+import concourse.mybir as mybir
+
+FLOPS = 603979776
+
+F32 = mybir.dt.float32
+BF16 = mybir.dt.bfloat16
+I32 = mybir.dt.int32
+U32 = mybir.dt.uint32
+U16 = mybir.dt.uint16
+U8 = mybir.dt.uint8
+E4M3 = mybir.dt.float8_e4m3fn_x4
+E5M2 = mybir.dt.float8_e5m2_x4
+E2M1 = mybir.dt.float4_e2m1fn_x4
+ACT = mybir.ActivationFunctionType
+ALU = mybir.AluOpType
+
+P = 128
+PACK = 4
+T, J, R, C, O, N, E = 1024, 256, 512, 512, 256, 256, 1024
+ROWS = 16
+TOP = P - ROWS
+HALF = O // 2
+
+XT0, XO0, W0, WB0 = 0, J, 2 * J, 2 * J + 2 * R
+PLANE = WB0 + N
+
+
+def tile_list_crossed_twoboards_one_finalgate_kernel(
+    tc, xt_words, xt_scales, xo_words, xo_scales, w_words, w_scales, w2_words, w2_scales,
+    wb_words, wb_scales, tz, so, bo, offs, offs2, offs3, offs4, offs5, offs6, offs7, out,
+):
+    nc = tc.nc
+    with ExitStack() as ctx:
+        sb = ctx.enter_context(tc.tile_pool(name="sb", bufs=1))
+        ps = ctx.enter_context(tc.psum_pool(name="ps", bufs=4))
+
+        def load_list(src, name):
+            tile = sb.tile([P, J // 16], U16, name=name)
+            nc.sync.dma_start(tile[:], src)
+            return tile
+
+        def load_bytes(dst, src):
+            nc.sync.dma_start(dst.bitcast(I32), src.bitcast(I32))
+
+        xt_s = sb.tile([P, T], U8, name="xt_s")
+        xo_s = sb.tile([P, T], U8, name="xo_s")
+        ww_s = sb.tile([P, 2 * R], U8, name="ww_s")
+        plane = sb.tile([P, PLANE], U8, name="plane", align_bytes=64)
+        for region in (xt_s[0:TOP, :], xo_s[0:TOP, :], ww_s[0:TOP, :], plane[0:TOP, WB0:PLANE]):
+            nc.vector.memset(region.bitcast(I32), 0)
+
+        xt_w = sb.tile([P, T], U16, name="xt_w")
+        xo_w = sb.tile([P, T], U32, name="xo_w")
+        w_raw = sb.tile([P, R], U32, name="w_raw")
+        w2_raw = sb.tile([P, R], U32, name="w2_raw")
+
+        l1 = load_list(offs, "l1")
+        l2 = load_list(offs2, "l2")
+        load_bytes(xt_s[TOP:P, :], xt_scales[0])
+        load_bytes(xo_s[TOP:P, :], xo_scales[0])
+        load_bytes(ww_s[TOP:P, 0:R], w_scales[0])
+        load_bytes(ww_s[TOP:P, R : 2 * R], w2_scales[0])
+        load_bytes(xt_w[:], xt_words[0])
+        load_bytes(xo_w[:], xo_words[0].rearrange("p n t -> p (n t)"))
+        load_bytes(plane[TOP:P, WB0:PLANE], wb_scales[0])
+        l4 = load_list(offs4, "l4")
+        l3 = load_list(offs3, "l3")
+        l7 = load_list(offs7, "l7")
+        load_bytes(w2_raw[:], w2_words[0].rearrange("p n t -> p (n t)"))
+        load_bytes(w_raw[:], w_words[0].rearrange("p n t -> p (n t)"))
+        l6 = load_list(offs6, "l6")
+        l5 = load_list(offs5, "l5")
+
+        xt_sg = sb.tile([P, J], U8, name="xt_sg")
+        xo_sg = sb.tile([P, J], U8, name="xo_sg")
+        nc.vector.tensor_copy(xt_sg[:], xt_s[:].indirect(l1[:]))
+        nc.vector.tensor_copy(xo_sg[:], xo_s[:].indirect(l2[:]))
+        nc.vector.tensor_copy(
+            out=plane[:, W0:WB0].rearrange("p (t c i) -> p c t i", t=PACK, i=16),
+            in_=ww_s[:].rearrange("p (c i t) -> p c t i", t=PACK, i=16),
+        )
+        nc.vector.tensor_copy(plane[:, XT0 : XT0 + J].bitcast(I32), xt_sg[:].bitcast(I32))
+        nc.vector.tensor_copy(plane[:, XO0 : XO0 + J].bitcast(I32), xo_sg[:].bitcast(I32))
+        for q in range(4):
+            queue = nc.scalar if q % 2 == 0 else nc.sync
+            queue.dma_start(
+                plane[32 * q : 32 * q + 4, :].bitcast(I32),
+                plane[TOP + 4 * q : TOP + 4 * q + 4, :].bitcast(I32),
+            )
+
+        xt_g = sb.tile([P, J], U16, name="xt_g", align_bytes=64)
+        xo_g = sb.tile([P, J], U32, name="xo_g", align_bytes=64)
+        nc.vector.tensor_copy(xt_g[:], xt_w[:].indirect(l1[:]))
+        nc.vector.tensor_copy(xo_g[:], xo_w[:].indirect(l2[:]))
+        w_d = sb.tile([P, R], U32, name="w_d", align_bytes=64)
+        w2_d = sb.tile([P, R], U32, name="w2_d", align_bytes=64)
+        for dealt, raw in ((w2_d, w2_raw), (w_d, w_raw)):
+            nc.vector.tensor_copy(
+                out=dealt[:].bitcast(I32).rearrange("p (t c i) -> p c t i", t=PACK, i=4),
+                in_=raw[:].bitcast(I32).rearrange("p (c i t) -> p c t i", t=PACK, i=4),
+            )
+
+        def load_gate_inputs(c, tags):
+            rows = slice(P * c, P * (c + 1))
+            tiles = []
+            for src, tag, name in zip((tz, so, bo), tags, ("tz", "so", "bo")):
+                tile = sb.tile([P, src.shape[1]], F32, name=f"{name}{c}", tag=tag)
+                nc.sync.dma_start(tile[:], src[rows, :])
+                tiles.append(tile)
+            return tiles
+
+        def look_up_gate(inputs, gate):
+            table, slope, offset = inputs
+            nc.scalar.activation(
+                out=gate[:], in_=table[:].indirect(l7[:]), func=ACT.Sigmoid, bias=offset[:], scale=slope[:]
+            )
+            return gate
+
+        def new_board(name, engine, tag):
+            board = sb.tile([P, C], F32, name=name, tag=tag)
+            engine.memset(board[:], 0.0)
+            return board
+
+        gate_in0 = load_gate_inputs(0, ("xt_sg", "xo_sg", "w2_raw"))
+        pv, pw = [], []
+        for t in range(2):
+            pv.append(new_board(f"pv{t}", nc.vector, f"pv{t}"))
+            pw.append(new_board(f"pw{t}", nc.vector, f"pw{t}"))
+        pv.append(new_board("pv2", nc.vector, "pv2"))
+        pw.append(new_board("pw2", nc.gpsimd, "w_raw"))
+
+        xt_op = (xt_g[:].bitcast(E2M1), plane[:, XT0 : XT0 + J])
+        xo_op = (xo_g[:].bitcast(E4M3), plane[:, XO0 : XO0 + J])
+
+        def first_stage(t, tag, weights):
+            acc = ps.tile([P, J], F32, name=tag, tag=tag)
+            for i, ((codes, fmt, which), (rhs, rhs_scale)) in enumerate(zip(weights, (xt_op, xo_op))):
+                s0 = W0 + 2 * P * t + P * which
+                nc.tensor.matmul_mx(
+                    out=acc[:], lhsT=codes[:, P * t : P * (t + 1)].bitcast(fmt),
+                    lhsT_scale=plane[:, s0 : s0 + P], rhs=rhs, rhs_scale=rhs_scale,
+                    start=(i == 0), stop=(i == 1),
+                )
+            return acc
+
+        w_op, w2_op = (w_d, E4M3, 0), (w2_d, E5M2, 1)
+        a_res, b_res = [], []
+        for t in range(PACK):
+            b_ps = first_stage(t, "b", (w2_op, w_op))
+            a_ps = first_stage(t, "a", (w_op, w2_op))
+            b_sb = sb.tile([P, J], F32, name=f"b_sb{t}", align_bytes=64)
+            a_sb = sb.tile([P, J], F32, name=f"a_sb{t}")
+            if t < 2:
+                nc.scalar.copy(b_sb[:], b_ps[:])
+            else:
+                nc.vector.tensor_copy(b_sb[:], b_ps[:])
+            nc.vector.tensor_copy(a_sb[:], a_ps[:])
+            a_res.append(a_sb)
+            b_res.append(b_sb)
+
+        diff = [sb.tile([P, 2, O], F32, name=f"diff{u}") for u in range(2)]
+        halves = [slice(HALF * h, HALF * (h + 1)) for h in range(2)]
+
+        def place_and_read(t):
+            nc.scalar.activation(pv[t][:].indirect(l4[:]), b_res[t][:], ACT.Copy)
+            nc.vector.tensor_copy(pw[t][:].indirect(l3[:]), a_res[t][:])
+            v_g = sb.tile([P, O], F32, name=f"v_g{t}")
+            nc.scalar.activation(v_g[:], pv[t][:].indirect(l6[:]), ACT.Copy)
+            d = diff[t // 2]
+            if t < PACK - 1:
+                nc.vector.tensor_tensor(d[:, t % 2, :], pw[t][:].indirect(l5[:]), v_g[:], ALU.subtract)
+            else:
+                for h in range(2):
+                    nc.vector.tensor_tensor(
+                        d[:, t % 2, halves[h]], pw[t][:].indirect(l5[:, 8 * h : 8 * h + 8]),
+                        v_g[:, halves[h]], ALU.subtract,
+                    )
+
+        place_and_read(0)
+        pw.append(new_board("pw3", nc.gpsimd, "a_sb0"))
+        b0_tag_board = sb.tile([P, C], F32, name="pv3", tag="b_sb0", align_bytes=64)
+        nc.gpsimd.memset(b0_tag_board[:], 0.0)
+        pv.append(b0_tag_board)
+        place_and_read(1)
+        gate_in1 = load_gate_inputs(1, ("a_sb1", "v_g0", "v_g1"))
+        wb_w = sb.tile([P, 2 * N], U8, name="wb_w", tag="b_sb1", align_bytes=64)
+        load_bytes(wb_w[:], wb_words[0])
+        place_and_read(2)
+        place_and_read(3)
+        gates = [look_up_gate(gate_in0, sb.tile([P, O], F32, name="gate0"))]
+
+        hid = sb.tile([P, O, PACK], BF16, name="hid", tag="b_sb2", align_bytes=64)
+
+        def magnitude(u, cols):
+            nc.scalar.activation(
+                out=hid[:, cols, 2 * u : 2 * u + 2],
+                in_=diff[u][:, :, cols].rearrange("p t o -> p o t"),
+                func=ACT.Abs,
+            )
+
+        magnitude(0, slice(0, O))
+        for cols in halves:
+            magnitude(1, cols)
+        gates.append(look_up_gate(gate_in1, sb.tile([P, O], F32, name="gate1", tag="diff1")))
+
+        hid_q = sb.tile([P, O], U32, name="hid_q", align_bytes=64)
+        hid_s = sb.tile([P, O], U8, name="hid_s", align_bytes=64)
+        out_v = out.rearrange("(c p) o -> p c o", p=P)
+        for h in range(2):
+            cols = halves[h]
+            nc.vector.quantize_mx(
+                out=hid_q[:, cols].bitcast(E5M2), scales=hid_s[:, cols],
+                in_=hid[:, cols, :].rearrange("p o t -> p (o t)"),
+            )
+            p_ps = ps.tile([P, 2, HALF], F32, name="p_ps", tag=("b", "a")[h])
+            for c in range(2):
+                nc.tensor.matmul_mx(
+                    out=p_ps[:, c, :], lhsT=wb_w[:, 2 * P * c : 2 * P * (c + 1)].bitcast(E2M1),
+                    lhsT_scale=plane[:, WB0 + P * c : WB0 + P * (c + 1)],
+                    rhs=hid_q[:, cols].bitcast(E5M2), rhs_scale=hid_s[:, cols], start=True, stop=True,
+                )
+            y = sb.tile([P, 2, HALF], F32, name=f"y{h}")
+            for c in range(2):
+                nc.vector.tensor_tensor(y[:, c, :], p_ps[:, c, :], gates[c][:, cols], ALU.mult)
+            nc.sync.dma_start(out_v[:, :, cols], y[:])

@@ -44,24 +44,29 @@ def tile_list_crossed_twoboards_one_finalgate_kernel(
         def load_bytes(dst, src):
             nc.sync.dma_start(dst.bitcast(I32), src.bitcast(I32))
 
+        warm_in = sb.tile([P, 1], F32, name="warm_in")
+        warm_out = sb.tile([P, 1], F32, name="warm_out")
+        nc.gpsimd.memset(warm_in[:], 0.0)
+        nc.scalar.activation(warm_out[:], warm_in[:], ACT.Sigmoid)
+
         xt_s = sb.tile([P, T], U8, name="xt_s")
         xo_s = sb.tile([P, T], U8, name="xo_s")
-        ww_s = sb.tile([P, 2 * R], U8, name="ww_s")
+        ww_s = sb.tile([P, 2 * R], U8, name="ww_s", align_bytes=64)
         plane = sb.tile([P, PLANE], U8, name="plane", align_bytes=64)
         for region in (xt_s[0:TOP, :], xo_s[0:TOP, :], ww_s[0:TOP, :], plane[0:TOP, WB0:PLANE]):
             nc.vector.memset(region.bitcast(I32), 0)
 
         xt_w = sb.tile([P, T], U16, name="xt_w")
         xo_w = sb.tile([P, T], U32, name="xo_w")
-        w_raw = sb.tile([P, R], U32, name="w_raw")
-        w2_raw = sb.tile([P, R], U32, name="w2_raw")
+        w_raw = sb.tile([P, R], U32, name="w_raw", align_bytes=64)
+        w2_raw = sb.tile([P, R], U32, name="w2_raw", align_bytes=64)
 
         l1 = load_list(offs, "l1")
-        l2 = load_list(offs2, "l2")
         load_bytes(xt_s[TOP:P, :], xt_scales[0])
-        load_bytes(xo_s[TOP:P, :], xo_scales[0])
         load_bytes(ww_s[TOP:P, 0:R], w_scales[0])
         load_bytes(ww_s[TOP:P, R : 2 * R], w2_scales[0])
+        l2 = load_list(offs2, "l2")
+        load_bytes(xo_s[TOP:P, :], xo_scales[0])
         load_bytes(xt_w[:], xt_words[0])
         load_bytes(xo_w[:], xo_words[0].rearrange("p n t -> p (n t)"))
         load_bytes(plane[TOP:P, WB0:PLANE], wb_scales[0])
@@ -73,25 +78,26 @@ def tile_list_crossed_twoboards_one_finalgate_kernel(
         l6 = load_list(offs6, "l6")
         l5 = load_list(offs5, "l5")
 
-        xt_sg = sb.tile([P, J], U8, name="xt_sg")
-        xo_sg = sb.tile([P, J], U8, name="xo_sg")
+        xt_sg = sb.tile([P, J], U8, name="xt_sg", align_bytes=64)
+        xo_sg = sb.tile([P, J], U8, name="xo_sg", align_bytes=64)
         nc.vector.tensor_copy(xt_sg[:], xt_s[:].indirect(l1[:]))
         nc.vector.tensor_copy(xo_sg[:], xo_s[:].indirect(l2[:]))
-        nc.vector.tensor_copy(
-            out=plane[:, W0:WB0].rearrange("p (t c i) -> p c t i", t=PACK, i=16),
-            in_=ww_s[:].rearrange("p (c i t) -> p c t i", t=PACK, i=16),
-        )
+        for which in range(2):
+            nc.gpsimd.tensor_copy(
+                out=plane[:, W0 + R * which : W0 + R * (which + 1)].rearrange("p (t c i) -> p c t i", t=PACK, i=16),
+                in_=ww_s[:, R * which : R * (which + 1)].rearrange("p (c i t) -> p c t i", t=PACK, i=16),
+            )
         nc.vector.tensor_copy(plane[:, XT0 : XT0 + J].bitcast(I32), xt_sg[:].bitcast(I32))
         nc.vector.tensor_copy(plane[:, XO0 : XO0 + J].bitcast(I32), xo_sg[:].bitcast(I32))
         for q in range(4):
-            queue = nc.scalar if q % 2 == 0 else nc.sync
+            queue = nc.scalar if q == 3 else nc.sync
             queue.dma_start(
                 plane[32 * q : 32 * q + 4, :].bitcast(I32),
                 plane[TOP + 4 * q : TOP + 4 * q + 4, :].bitcast(I32),
             )
 
-        xt_g = sb.tile([P, J], U16, name="xt_g", align_bytes=64)
-        xo_g = sb.tile([P, J], U32, name="xo_g", align_bytes=64)
+        xt_g = sb.tile([P, J], U16, name="xt_g", tag="xt_sg", align_bytes=64)
+        xo_g = sb.tile([P, J], U32, name="xo_g", tag="xo_sg", align_bytes=64)
         nc.vector.tensor_copy(xt_g[:], xt_w[:].indirect(l1[:]))
         nc.vector.tensor_copy(xo_g[:], xo_w[:].indirect(l2[:]))
         w_d = sb.tile([P, R], U32, name="w_d", align_bytes=64)
@@ -102,33 +108,30 @@ def tile_list_crossed_twoboards_one_finalgate_kernel(
                 in_=raw[:].bitcast(I32).rearrange("p (c i t) -> p c t i", t=PACK, i=4),
             )
 
-        def load_gate_inputs(c, tags):
-            rows = slice(P * c, P * (c + 1))
-            tiles = []
-            for src, tag, name in zip((tz, so, bo), tags, ("tz", "so", "bo")):
-                tile = sb.tile([P, src.shape[1]], F32, name=f"{name}{c}", tag=tag)
-                nc.sync.dma_start(tile[:], src[rows, :])
-                tiles.append(tile)
-            return tiles
+        slope = sb.tile([P, 2], F32, name="slope", tag="xt_w")
+        offset = sb.tile([P, 2], F32, name="offset", tag="xo_w")
+        with nc.allow_non_contiguous_dma(reason="one value a partition and output tile"):
+            nc.sync.dma_start(slope[:], so.rearrange("(c p) o -> p (c o)", p=P))
+            nc.sync.dma_start(offset[:], bo.rearrange("(c p) o -> p (c o)", p=P))
 
-        def look_up_gate(inputs, gate):
-            table, slope, offset = inputs
+        def look_up_gate(c, table, tag):
+            gate = sb.tile([P, O], F32, name=f"gate{c}", tag=tag, align_bytes=64)
             nc.scalar.activation(
-                out=gate[:], in_=table[:].indirect(l7[:]), func=ACT.Sigmoid, bias=offset[:], scale=slope[:]
+                out=gate[:], in_=table[:].indirect(l7[:]), func=ACT.Sigmoid,
+                bias=offset[:, c : c + 1], scale=slope[:, c : c + 1],
             )
             return gate
 
         def new_board(name, engine, tag):
-            board = sb.tile([P, C], F32, name=name, tag=tag)
+            board = sb.tile([P, C], F32, name=name, tag=tag, align_bytes=64)
             engine.memset(board[:], 0.0)
             return board
 
-        gate_in0 = load_gate_inputs(0, ("xt_sg", "xo_sg", "w2_raw"))
         pv, pw = [], []
         for t in range(2):
-            pv.append(new_board(f"pv{t}", nc.vector, f"pv{t}"))
-            pw.append(new_board(f"pw{t}", nc.vector, f"pw{t}"))
-        pv.append(new_board("pv2", nc.vector, "pv2"))
+            pv.append(new_board(f"pv{t}", nc.vector if t == 0 else nc.gpsimd, f"pv{t}"))
+            pw.append(new_board(f"pw{t}", nc.gpsimd, f"pw{t}"))
+        pv.append(new_board("pv2", nc.gpsimd, "pv2"))
         pw.append(new_board("pw2", nc.gpsimd, "w_raw"))
 
         xt_op = (xt_g[:].bitcast(E2M1), plane[:, XT0 : XT0 + J])
@@ -137,7 +140,7 @@ def tile_list_crossed_twoboards_one_finalgate_kernel(
         def first_stage(t, tag, weights):
             acc = ps.tile([P, J], F32, name=tag, tag=tag)
             for i, ((codes, fmt, which), (rhs, rhs_scale)) in enumerate(zip(weights, (xt_op, xo_op))):
-                s0 = W0 + 2 * P * t + P * which
+                s0 = W0 + R * which + P * t
                 nc.tensor.matmul_mx(
                     out=acc[:], lhsT=codes[:, P * t : P * (t + 1)].bitcast(fmt),
                     lhsT_scale=plane[:, s0 : s0 + P], rhs=rhs, rhs_scale=rhs_scale,
@@ -146,52 +149,66 @@ def tile_list_crossed_twoboards_one_finalgate_kernel(
             return acc
 
         w_op, w2_op = (w_d, E4M3, 0), (w2_d, E5M2, 1)
-        a_res, b_res = [], []
+        sums = []
         for t in range(PACK):
             b_ps = first_stage(t, "b", (w2_op, w_op))
             a_ps = first_stage(t, "a", (w_op, w2_op))
-            b_sb = sb.tile([P, J], F32, name=f"b_sb{t}", align_bytes=64)
-            a_sb = sb.tile([P, J], F32, name=f"a_sb{t}")
-            if t < 2:
-                nc.scalar.copy(b_sb[:], b_ps[:])
-            else:
-                nc.vector.tensor_copy(b_sb[:], b_ps[:])
-            nc.vector.tensor_copy(a_sb[:], a_ps[:])
-            a_res.append(a_sb)
-            b_res.append(b_sb)
+            sums.append((a_ps, b_ps))
 
-        diff = [sb.tile([P, 2, O], F32, name=f"diff{u}") for u in range(2)]
+        diff = [sb.tile([P, 2, O], F32, name=f"diff{u}", align_bytes=64) for u in range(2)]
         halves = [slice(HALF * h, HALF * (h + 1)) for h in range(2)]
+        results = []
 
-        def place_and_read(t):
-            nc.scalar.activation(pv[t][:].indirect(l4[:]), b_res[t][:], ACT.Copy)
-            nc.vector.tensor_copy(pw[t][:].indirect(l3[:]), a_res[t][:])
-            v_g = sb.tile([P, O], F32, name=f"v_g{t}")
-            nc.scalar.activation(v_g[:], pv[t][:].indirect(l6[:]), ACT.Copy)
-            d = diff[t // 2]
-            if t < PACK - 1:
-                nc.vector.tensor_tensor(d[:, t % 2, :], pw[t][:].indirect(l5[:]), v_g[:], ALU.subtract)
+        def leave_psum(t):
+            a_sb = sb.tile([P, J], F32, name=f"a_sb{t}", align_bytes=64)
+            b_sb = sb.tile([P, J], F32, name=f"b_sb{t}", align_bytes=64)
+            if t == PACK - 1:
+                nc.vector.tensor_copy(b_sb[:], sums[t][1][:])
             else:
-                for h in range(2):
-                    nc.vector.tensor_tensor(
-                        d[:, t % 2, halves[h]], pw[t][:].indirect(l5[:, 8 * h : 8 * h + 8]),
-                        v_g[:, halves[h]], ALU.subtract,
-                    )
+                nc.scalar.copy(b_sb[:], sums[t][1][:])
+            nc.vector.tensor_copy(a_sb[:], sums[t][0][:])
+            results.append((a_sb, b_sb))
 
-        place_and_read(0)
+        def place(t):
+            nc.scalar.activation(pv[t][:].indirect(l4[:]), results[t][1][:], ACT.Copy)
+            nc.vector.tensor_copy(pw[t][:].indirect(l3[:]), results[t][0][:])
+
+        def read(t, pieces):
+            v_g = sb.tile([P, O], F32, name=f"v_g{t}", align_bytes=64)
+            for cols in pieces:
+                entries = slice(cols.start // 16, cols.stop // 16)
+                nc.scalar.activation(v_g[:, cols], pv[t][:].indirect(l6[:, entries]), ACT.Copy)
+                nc.vector.tensor_tensor(
+                    diff[t // 2][:, t % 2, cols], pw[t][:].indirect(l5[:, entries]), v_g[:, cols], ALU.subtract
+                )
+
+        def load_table(c, tag):
+            table = sb.tile([P, E], F32, name=f"tz{c}", tag=tag, align_bytes=64)
+            nc.sync.dma_start(table[:], tz[P * c : P * (c + 1), :])
+            return table
+
+        whole = [slice(0, O)]
+        tz0 = load_table(0, "w2_raw")
+        leave_psum(0)
+        place(0)
+        leave_psum(1)
+        read(0, whole)
         pw.append(new_board("pw3", nc.gpsimd, "a_sb0"))
-        b0_tag_board = sb.tile([P, C], F32, name="pv3", tag="b_sb0", align_bytes=64)
-        nc.gpsimd.memset(b0_tag_board[:], 0.0)
-        pv.append(b0_tag_board)
-        place_and_read(1)
-        gate_in1 = load_gate_inputs(1, ("a_sb1", "v_g0", "v_g1"))
+        pv.append(new_board("pv3", nc.gpsimd, "v_g0"))
+        place(1)
+        leave_psum(2)
+        read(1, whole)
+        tz1 = load_table(1, "a_sb1")
         wb_w = sb.tile([P, 2 * N], U8, name="wb_w", tag="b_sb1", align_bytes=64)
         load_bytes(wb_w[:], wb_words[0])
-        place_and_read(2)
-        place_and_read(3)
-        gates = [look_up_gate(gate_in0, sb.tile([P, O], F32, name="gate0"))]
+        leave_psum(3)
+        place(2)
+        gates = [look_up_gate(0, tz0, "v_g1")]
+        read(2, whole)
+        place(3)
+        read(3, halves)
 
-        hid = sb.tile([P, O, PACK], BF16, name="hid", tag="b_sb2", align_bytes=64)
+        hid = sb.tile([P, O, PACK], BF16, name="hid", tag="b_sb3", align_bytes=64)
 
         def magnitude(u, cols):
             nc.scalar.activation(
@@ -203,25 +220,26 @@ def tile_list_crossed_twoboards_one_finalgate_kernel(
         magnitude(0, slice(0, O))
         for cols in halves:
             magnitude(1, cols)
-        gates.append(look_up_gate(gate_in1, sb.tile([P, O], F32, name="gate1", tag="diff1")))
+        gates.append(look_up_gate(1, tz1, "diff1"))
 
         hid_q = sb.tile([P, O], U32, name="hid_q", align_bytes=64)
         hid_s = sb.tile([P, O], U8, name="hid_s", align_bytes=64)
-        out_v = out.rearrange("(c p) o -> p c o", p=P)
+        p_ps = []
         for h in range(2):
             cols = halves[h]
             nc.vector.quantize_mx(
                 out=hid_q[:, cols].bitcast(E5M2), scales=hid_s[:, cols],
                 in_=hid[:, cols, :].rearrange("p o t -> p (o t)"),
             )
-            p_ps = ps.tile([P, 2, HALF], F32, name="p_ps", tag=("b", "a")[h])
+            p_ps.append(ps.tile([P, 2, HALF], F32, name="p_ps", tag=("b", "a")[h]))
             for c in range(2):
                 nc.tensor.matmul_mx(
-                    out=p_ps[:, c, :], lhsT=wb_w[:, 2 * P * c : 2 * P * (c + 1)].bitcast(E2M1),
+                    out=p_ps[h][:, c, :], lhsT=wb_w[:, 2 * P * c : 2 * P * (c + 1)].bitcast(E2M1),
                     lhsT_scale=plane[:, WB0 + P * c : WB0 + P * (c + 1)],
                     rhs=hid_q[:, cols].bitcast(E5M2), rhs_scale=hid_s[:, cols], start=True, stop=True,
                 )
-            y = sb.tile([P, 2, HALF], F32, name=f"y{h}")
-            for c in range(2):
-                nc.vector.tensor_tensor(y[:, c, :], p_ps[:, c, :], gates[c][:, cols], ALU.mult)
-            nc.sync.dma_start(out_v[:, :, cols], y[:])
+        for c in range(2):
+            y = sb.tile([P, O], F32, name=f"y{c}")
+            for h in range(2):
+                nc.vector.tensor_tensor(y[:, halves[h]], p_ps[h][:, c, :], gates[c][:, halves[h]], ALU.mult)
+            nc.sync.dma_start(out[P * c : P * (c + 1), :], y[:])

@@ -44,11 +44,6 @@ def tile_list_crossed_twoboards_one_finalgate_kernel(
         def load_bytes(dst, src):
             nc.sync.dma_start(dst.bitcast(I32), src.bitcast(I32))
 
-        warm_in = sb.tile([P, 1], F32, name="warm_in")
-        warm_out = sb.tile([P, 1], F32, name="warm_out")
-        nc.gpsimd.memset(warm_in[:], 0.0)
-        nc.scalar.activation(warm_out[:], warm_in[:], ACT.Sigmoid)
-
         xt_s = sb.tile([P, T], U8, name="xt_s")
         xo_s = sb.tile([P, T], U8, name="xo_s")
         ww_s = sb.tile([P, 2 * R], U8, name="ww_s", align_bytes=64)
@@ -56,8 +51,13 @@ def tile_list_crossed_twoboards_one_finalgate_kernel(
         for region in (xt_s[0:TOP, :], xo_s[0:TOP, :], ww_s[0:TOP, :], plane[0:TOP, WB0:PLANE]):
             nc.vector.memset(region.bitcast(I32), 0)
 
+        warm_in = sb.tile([P, 1], F32, name="warm_in")
+        warm_out = sb.tile([P, 1], F32, name="warm_out")
+        nc.vector.memset(warm_in[:], 0.0)
+        nc.scalar.activation(warm_out[:], warm_in[:], ACT.Sigmoid)
+
         xt_w = sb.tile([P, T], U16, name="xt_w")
-        xo_w = sb.tile([P, T], U32, name="xo_w")
+        xo_w = sb.tile([P, T], U32, name="xo_w", align_bytes=64)
         w_raw = sb.tile([P, R], U32, name="w_raw", align_bytes=64)
         w2_raw = sb.tile([P, R], U32, name="w2_raw", align_bytes=64)
 
@@ -83,7 +83,7 @@ def tile_list_crossed_twoboards_one_finalgate_kernel(
         nc.vector.tensor_copy(xt_sg[:], xt_s[:].indirect(l1[:]))
         nc.vector.tensor_copy(xo_sg[:], xo_s[:].indirect(l2[:]))
         for which in range(2):
-            nc.gpsimd.tensor_copy(
+            nc.vector.tensor_copy(
                 out=plane[:, W0 + R * which : W0 + R * (which + 1)].rearrange("p (t c i) -> p c t i", t=PACK, i=16),
                 in_=ww_s[:, R * which : R * (which + 1)].rearrange("p (c i t) -> p c t i", t=PACK, i=16),
             )
@@ -108,12 +108,6 @@ def tile_list_crossed_twoboards_one_finalgate_kernel(
                 in_=raw[:].bitcast(I32).rearrange("p (c i t) -> p c t i", t=PACK, i=4),
             )
 
-        slope = sb.tile([P, 2], F32, name="slope", tag="xt_w")
-        offset = sb.tile([P, 2], F32, name="offset", tag="xo_w")
-        with nc.allow_non_contiguous_dma(reason="one value a partition and output tile"):
-            nc.sync.dma_start(slope[:], so.rearrange("(c p) o -> p (c o)", p=P))
-            nc.sync.dma_start(offset[:], bo.rearrange("(c p) o -> p (c o)", p=P))
-
         def look_up_gate(c, table, tag):
             gate = sb.tile([P, O], F32, name=f"gate{c}", tag=tag, align_bytes=64)
             nc.scalar.activation(
@@ -128,11 +122,9 @@ def tile_list_crossed_twoboards_one_finalgate_kernel(
             return board
 
         pv, pw = [], []
-        for t in range(2):
-            pv.append(new_board(f"pv{t}", nc.vector if t == 0 else nc.gpsimd, f"pv{t}"))
-            pw.append(new_board(f"pw{t}", nc.gpsimd, f"pw{t}"))
-        pv.append(new_board("pv2", nc.gpsimd, "pv2"))
-        pw.append(new_board("pw2", nc.gpsimd, "w_raw"))
+        for t in range(PACK):
+            pv.append(new_board(f"pv{t}", nc.vector, "xo_w" if t == PACK - 1 else f"pv{t}"))
+            pw.append(new_board(f"pw{t}", nc.vector, "w_raw" if t == PACK - 1 else f"pw{t}"))
 
         xt_op = (xt_g[:].bitcast(E2M1), plane[:, XT0 : XT0 + J])
         xo_op = (xo_g[:].bitcast(E4M3), plane[:, XO0 : XO0 + J])
@@ -155,7 +147,7 @@ def tile_list_crossed_twoboards_one_finalgate_kernel(
             a_ps = first_stage(t, "a", (w_op, w2_op))
             sums.append((a_ps, b_ps))
 
-        diff = [sb.tile([P, 2, O], F32, name=f"diff{u}", align_bytes=64) for u in range(2)]
+        diff = sb.tile([P, PACK, O], F32, name="diff", align_bytes=64)
         halves = [slice(HALF * h, HALF * (h + 1)) for h in range(2)]
         results = []
 
@@ -179,7 +171,7 @@ def tile_list_crossed_twoboards_one_finalgate_kernel(
                 entries = slice(cols.start // 16, cols.stop // 16)
                 nc.scalar.activation(v_g[:, cols], pv[t][:].indirect(l6[:, entries]), ACT.Copy)
                 nc.vector.tensor_tensor(
-                    diff[t // 2][:, t % 2, cols], pw[t][:].indirect(l5[:, entries]), v_g[:, cols], ALU.subtract
+                    diff[:, t, cols], pw[t][:].indirect(l5[:, entries]), v_g[:, cols], ALU.subtract
                 )
 
         def load_table(c, tag):
@@ -193,8 +185,12 @@ def tile_list_crossed_twoboards_one_finalgate_kernel(
         place(0)
         leave_psum(1)
         read(0, whole)
-        pw.append(new_board("pw3", nc.gpsimd, "a_sb0"))
-        pv.append(new_board("pv3", nc.gpsimd, "v_g0"))
+        slope = sb.tile([P, 2], F32, name="slope", tag="a_sb0", align_bytes=64)
+        offset = sb.tile([P, 2], F32, name="offset", tag="b_sb0", align_bytes=64)
+        with nc.allow_non_contiguous_dma(reason="one value a partition and output tile"):
+            nc.sync.dma_start(slope[:], so.rearrange("(c p) o -> p (c o)", p=P))
+            nc.sync.dma_start(offset[:], bo.rearrange("(c p) o -> p (c o)", p=P))
+
         place(1)
         leave_psum(2)
         read(1, whole)
@@ -208,19 +204,14 @@ def tile_list_crossed_twoboards_one_finalgate_kernel(
         place(3)
         read(3, halves)
 
-        hid = sb.tile([P, O, PACK], BF16, name="hid", tag="b_sb3", align_bytes=64)
-
-        def magnitude(u, cols):
+        hid = sb.tile([P, O, PACK], BF16, name="hid", align_bytes=64)
+        for cols in halves:
             nc.scalar.activation(
-                out=hid[:, cols, 2 * u : 2 * u + 2],
-                in_=diff[u][:, :, cols].rearrange("p t o -> p o t"),
+                out=hid[:, cols, :].rearrange("p (c i) t -> p c t i", i=4),
+                in_=diff[:, :, cols].rearrange("p t (c i) -> p c t i", i=4),
                 func=ACT.Abs,
             )
-
-        magnitude(0, slice(0, O))
-        for cols in halves:
-            magnitude(1, cols)
-        gates.append(look_up_gate(1, tz1, "diff1"))
+        gates.append(look_up_gate(1, tz1, "diff"))
 
         hid_q = sb.tile([P, O], U32, name="hid_q", align_bytes=64)
         hid_s = sb.tile([P, O], U8, name="hid_s", align_bytes=64)

from contextlib import ExitStack

import concourse.mybir as mybir

FLOPS = 603979776

F32 = mybir.dt.float32
BF16 = mybir.dt.bfloat16
I32 = mybir.dt.int32
U32 = mybir.dt.uint32
U16 = mybir.dt.uint16
U8 = mybir.dt.uint8
E4M3 = mybir.dt.float8_e4m3fn_x4
E5M2 = mybir.dt.float8_e5m2_x4
E2M1 = mybir.dt.float4_e2m1fn_x4
ACT = mybir.ActivationFunctionType
ALU = mybir.AluOpType

P = 128
PACK = 4
T, J, R, C, O, N, E = 1024, 256, 512, 512, 256, 256, 1024
ROWS = 16
TOP = P - ROWS
HALF = O // 2

XT0, XO0, W0, WB0 = 0, J, 2 * J, 2 * J + 2 * R
PLANE = WB0 + N


def tile_list_crossed_twoboards_one_finalgate_kernel(
    tc, xt_words, xt_scales, xo_words, xo_scales, w_words, w_scales, w2_words, w2_scales,
    wb_words, wb_scales, tz, so, bo, offs, offs2, offs3, offs4, offs5, offs6, offs7, out,
):
    nc = tc.nc
    with ExitStack() as ctx:
        sb = ctx.enter_context(tc.tile_pool(name="sb", bufs=1))
        ps = ctx.enter_context(tc.psum_pool(name="ps", bufs=4))

        def load_list(src, name):
            tile = sb.tile([P, J // 16], U16, name=name)
            nc.sync.dma_start(tile[:], src)
            return tile

        def load_bytes(dst, src):
            nc.sync.dma_start(dst.bitcast(I32), src.bitcast(I32))

        xt_s = sb.tile([P, T], U8, name="xt_s")
        xo_s = sb.tile([P, T], U8, name="xo_s")
        ww_s = sb.tile([P, 2 * R], U8, name="ww_s", align_bytes=64)
        plane = sb.tile([P, PLANE], U8, name="plane", align_bytes=64)
        for region in (xt_s[0:TOP, :], xo_s[0:TOP, :], ww_s[0:TOP, :], plane[0:TOP, WB0:PLANE]):
            nc.vector.memset(region.bitcast(I32), 0)

        warm_in = sb.tile([P, 1], F32, name="warm_in")
        warm_out = sb.tile([P, 1], F32, name="warm_out")
        nc.vector.memset(warm_in[:], 0.0)
        nc.scalar.activation(warm_out[:], warm_in[:], ACT.Sigmoid)

        xt_w = sb.tile([P, T], U16, name="xt_w")
        xo_w = sb.tile([P, T], U32, name="xo_w", align_bytes=64)
        w_raw = sb.tile([P, R], U32, name="w_raw", align_bytes=64)
        w2_raw = sb.tile([P, R], U32, name="w2_raw", align_bytes=64)

        l1 = load_list(offs, "l1")
        load_bytes(xt_s[TOP:P, :], xt_scales[0])
        load_bytes(ww_s[TOP:P, 0:R], w_scales[0])
        load_bytes(ww_s[TOP:P, R : 2 * R], w2_scales[0])
        l2 = load_list(offs2, "l2")
        load_bytes(xo_s[TOP:P, :], xo_scales[0])
        load_bytes(xt_w[:], xt_words[0])
        load_bytes(xo_w[:], xo_words[0].rearrange("p n t -> p (n t)"))
        load_bytes(plane[TOP:P, WB0:PLANE], wb_scales[0])
        l4 = load_list(offs4, "l4")
        l3 = load_list(offs3, "l3")
        l7 = load_list(offs7, "l7")
        load_bytes(w2_raw[:], w2_words[0].rearrange("p n t -> p (n t)"))
        load_bytes(w_raw[:], w_words[0].rearrange("p n t -> p (n t)"))
        l6 = load_list(offs6, "l6")
        l5 = load_list(offs5, "l5")

        xt_sg = sb.tile([P, J], U8, name="xt_sg", align_bytes=64)
        xo_sg = sb.tile([P, J], U8, name="xo_sg", align_bytes=64)
        nc.vector.tensor_copy(xt_sg[:], xt_s[:].indirect(l1[:]))
        nc.vector.tensor_copy(xo_sg[:], xo_s[:].indirect(l2[:]))
        for which in range(2):
            nc.vector.tensor_copy(
                out=plane[:, W0 + R * which : W0 + R * (which + 1)].rearrange("p (t c i) -> p c t i", t=PACK, i=16),
                in_=ww_s[:, R * which : R * (which + 1)].rearrange("p (c i t) -> p c t i", t=PACK, i=16),
            )
        nc.vector.tensor_copy(plane[:, XT0 : XT0 + J].bitcast(I32), xt_sg[:].bitcast(I32))
        nc.vector.tensor_copy(plane[:, XO0 : XO0 + J].bitcast(I32), xo_sg[:].bitcast(I32))
        for q in range(4):
            queue = nc.scalar if q == 3 else nc.sync
            queue.dma_start(
                plane[32 * q : 32 * q + 4, :].bitcast(I32),
                plane[TOP + 4 * q : TOP + 4 * q + 4, :].bitcast(I32),
            )

        xt_g = sb.tile([P, J], U16, name="xt_g", tag="xt_sg", align_bytes=64)
        xo_g = sb.tile([P, J], U32, name="xo_g", tag="xo_sg", align_bytes=64)
        nc.vector.tensor_copy(xt_g[:], xt_w[:].indirect(l1[:]))
        nc.vector.tensor_copy(xo_g[:], xo_w[:].indirect(l2[:]))
        w_d = sb.tile([P, R], U32, name="w_d", align_bytes=64)
        w2_d = sb.tile([P, R], U32, name="w2_d", align_bytes=64)
        for dealt, raw in ((w2_d, w2_raw), (w_d, w_raw)):
            nc.vector.tensor_copy(
                out=dealt[:].bitcast(I32).rearrange("p (t c i) -> p c t i", t=PACK, i=4),
                in_=raw[:].bitcast(I32).rearrange("p (c i t) -> p c t i", t=PACK, i=4),
            )

        def look_up_gate(c, table, tag):
            gate = sb.tile([P, O], F32, name=f"gate{c}", tag=tag, align_bytes=64)
            nc.scalar.activation(
                out=gate[:], in_=table[:].indirect(l7[:]), func=ACT.Sigmoid,
                bias=offset[:, c : c + 1], scale=slope[:, c : c + 1],
            )
            return gate

        def new_board(name, engine, tag):
            board = sb.tile([P, C], F32, name=name, tag=tag, align_bytes=64)
            engine.memset(board[:], 0.0)
            return board

        pv, pw = [], []
        for t in range(PACK):
            pv.append(new_board(f"pv{t}", nc.vector, "xo_w" if t == PACK - 1 else f"pv{t}"))
            pw.append(new_board(f"pw{t}", nc.vector, "w_raw" if t == PACK - 1 else f"pw{t}"))

        xt_op = (xt_g[:].bitcast(E2M1), plane[:, XT0 : XT0 + J])
        xo_op = (xo_g[:].bitcast(E4M3), plane[:, XO0 : XO0 + J])

        def first_stage(t, tag, weights):
            acc = ps.tile([P, J], F32, name=tag, tag=tag)
            for i, ((codes, fmt, which), (rhs, rhs_scale)) in enumerate(zip(weights, (xt_op, xo_op))):
                s0 = W0 + R * which + P * t
                nc.tensor.matmul_mx(
                    out=acc[:], lhsT=codes[:, P * t : P * (t + 1)].bitcast(fmt),
                    lhsT_scale=plane[:, s0 : s0 + P], rhs=rhs, rhs_scale=rhs_scale,
                    start=(i == 0), stop=(i == 1),
                )
            return acc

        w_op, w2_op = (w_d, E4M3, 0), (w2_d, E5M2, 1)
        sums = []
        for t in range(PACK):
            b_ps = first_stage(t, "b", (w2_op, w_op))
            a_ps = first_stage(t, "a", (w_op, w2_op))
            sums.append((a_ps, b_ps))

        diff = sb.tile([P, PACK, O], F32, name="diff", align_bytes=64)
        halves = [slice(HALF * h, HALF * (h + 1)) for h in range(2)]
        results = []

        def leave_psum(t):
            a_sb = sb.tile([P, J], F32, name=f"a_sb{t}", align_bytes=64)
            b_sb = sb.tile([P, J], F32, name=f"b_sb{t}", align_bytes=64)
            if t == PACK - 1:
                nc.vector.tensor_copy(b_sb[:], sums[t][1][:])
            else:
                nc.scalar.copy(b_sb[:], sums[t][1][:])
            nc.vector.tensor_copy(a_sb[:], sums[t][0][:])
            results.append((a_sb, b_sb))

        def place(t):
            nc.scalar.activation(pv[t][:].indirect(l4[:]), results[t][1][:], ACT.Copy)
            nc.vector.tensor_copy(pw[t][:].indirect(l3[:]), results[t][0][:])

        def read(t, pieces):
            v_g = sb.tile([P, O], F32, name=f"v_g{t}", align_bytes=64)
            for cols in pieces:
                entries = slice(cols.start // 16, cols.stop // 16)
                nc.scalar.activation(v_g[:, cols], pv[t][:].indirect(l6[:, entries]), ACT.Copy)
                nc.vector.tensor_tensor(
                    diff[:, t, cols], pw[t][:].indirect(l5[:, entries]), v_g[:, cols], ALU.subtract
                )

        def load_table(c, tag):
            table = sb.tile([P, E], F32, name=f"tz{c}", tag=tag, align_bytes=64)
            nc.sync.dma_start(table[:], tz[P * c : P * (c + 1), :])
            return table

        whole = [slice(0, O)]
        tz0 = load_table(0, "w2_raw")
        leave_psum(0)
        place(0)
        leave_psum(1)
        read(0, whole)
        slope = sb.tile([P, 2], F32, name="slope", tag="a_sb0", align_bytes=64)
        offset = sb.tile([P, 2], F32, name="offset", tag="b_sb0", align_bytes=64)
        with nc.allow_non_contiguous_dma(reason="one value a partition and output tile"):
            nc.sync.dma_start(slope[:], so.rearrange("(c p) o -> p (c o)", p=P))
            nc.sync.dma_start(offset[:], bo.rearrange("(c p) o -> p (c o)", p=P))

        place(1)
        leave_psum(2)
        read(1, whole)
        tz1 = load_table(1, "a_sb1")
        wb_w = sb.tile([P, 2 * N], U8, name="wb_w", tag="b_sb1", align_bytes=64)
        load_bytes(wb_w[:], wb_words[0])
        leave_psum(3)
        place(2)
        gates = [look_up_gate(0, tz0, "v_g1")]
        read(2, whole)
        place(3)
        read(3, halves)

        hid = sb.tile([P, O, PACK], BF16, name="hid", align_bytes=64)
        for cols in halves:
            nc.scalar.activation(
                out=hid[:, cols, :].rearrange("p (c i) t -> p c t i", i=4),
                in_=diff[:, :, cols].rearrange("p t (c i) -> p c t i", i=4),
                func=ACT.Abs,
            )
        gates.append(look_up_gate(1, tz1, "diff"))

        hid_q = sb.tile([P, O], U32, name="hid_q", align_bytes=64)
        hid_s = sb.tile([P, O], U8, name="hid_s", align_bytes=64)
        p_ps = []
        for h in range(2):
            cols = halves[h]
            nc.vector.quantize_mx(
                out=hid_q[:, cols].bitcast(E5M2), scales=hid_s[:, cols],
                in_=hid[:, cols, :].rearrange("p o t -> p (o t)"),
            )
            p_ps.append(ps.tile([P, 2, HALF], F32, name="p_ps", tag=("b", "a")[h]))
            for c in range(2):
                nc.tensor.matmul_mx(
                    out=p_ps[h][:, c, :], lhsT=wb_w[:, 2 * P * c : 2 * P * (c + 1)].bitcast(E2M1),
                    lhsT_scale=plane[:, WB0 + P * c : WB0 + P * (c + 1)],
                    rhs=hid_q[:, cols].bitcast(E5M2), rhs_scale=hid_s[:, cols], start=True, stop=True,
                )
        for c in range(2):
            y = sb.tile([P, O], F32, name=f"y{c}")
            for h in range(2):
                nc.vector.tensor_tensor(y[:, halves[h]], p_ps[h][:, c, :], gates[c][:, halves[h]], ALU.mult)
            nc.sync.dma_start(out[P * c : P * (c + 1), :], y[:])
